import numpy as np
CORES = [5,13,21,29,37,45,53,61,69,77,85,93,101,109,117,125]
N = 16
WIDTHS = [1,2,4,4,4,4,1,1,1,1,2,4,1,1,1,1]
XW = 4
def setup_inputs(rng):
    return {"x": rng.standard_normal((N, 128, XW), dtype=np.float32)}
def reference(x):
    g = np.concatenate([x[r][:, :WIDTHS[r]] for r in range(N)], axis=1)
    return {"y": np.broadcast_to(g, (N,) + g.shape)}

@@ -1,0 +1,76 @@
+from concourse.bass import DstId, RemoteDMATransfer
+
+SCRATCH = {
+    "land": ("sbuf", [128, 33], "float32"),
+    "stage": ("sbuf", [128, 4], "float32"),
+    "relay": ("sbuf", [128, 4], "float32"),
+}
+SEMAPHORES = ["loaded", "copied", "arrived", "sent", "stored"]
+
+LOW8 = 0x00FF
+HIGH8 = 0xFF00
+RELAY_CORE = 6
+
+
+def _dst(topo, c):
+    rid, pid, _se = topo.addr(c)
+    return DstId(rid=rid, pnc=pid)
+
+
+def rank_program(g, core, T, topo):
+    widths = T.tables["WIDTHS"]
+    cores = list(T.cores)
+    off = [sum(widths[:r]) for r in range(len(cores))]
+    chip = topo.chip(core)
+    rank = T.rank_of(core)
+
+    if rank is None:
+        if core % 8 != RELAY_CORE:
+            return
+        owners = [r for r, c in enumerate(cores) if topo.chip(c) == chip]
+        if not owners:
+            return
+        r = owners[0]
+        w, o = widths[r], off[r]
+        far = [c for c in cores if (topo.chip(c) & 1) != (chip & 1)]
+        g.wait_ge(T.sem.arrived, 8)
+        g.remote_dma_fused(
+            [RemoteDMATransfer(src=T.relay[:, 0:w],
+                               dsts=[T.land[:, o:o + w] for _ in far],
+                               dst_ids=[_dst(topo, c) for c in far],
+                               dma_engine_mask=LOW8, remote_sem=T.sem.arrived)],
+            local_sem=T.sem.sent)
+        g.wait_ge(T.sem.sent, 8)
+        return
+
+    w, o = widths[rank], off[rank]
+    mine = T.land[:, o:o + w]
+    if w >= 2:
+        g.sync.dma_start(mine, T.x[:, 0:w]).then_inc(T.sem.loaded, 16)
+        src = mine
+    else:
+        g.sync.dma_start(T.stage[:], T.x[:]).then_inc(T.sem.loaded, 16)
+        src = T.stage[:, 0:1]
+        g.scalar.wait_ge(T.sem.loaded, 16)
+        g.scalar.dma_start(mine, src).then_inc(T.sem.copied, 16)
+
+    near = [c for c in cores if c != core and (topo.chip(c) & 1) == (chip & 1)]
+    relay = chip * 8 + RELAY_CORE
+    g.wait_ge(T.sem.loaded, 16)
+    g.remote_dma_fused(
+        [RemoteDMATransfer(src=src, dst=T.relay[:, 0:w], dst_ids=[_dst(topo, relay)],
+                           dma_engine_mask=HIGH8, remote_sem=T.sem.arrived),
+         RemoteDMATransfer(src=src,
+                           dsts=[T.land[:, o:o + w] for _ in near],
+                           dst_ids=[_dst(topo, c) for c in near],
+                           dma_engine_mask=LOW8, remote_sem=T.sem.arrived)],
+        local_sem=T.sem.sent)
+
+    g.sync.wait_ge(T.sem.loaded, 16)
+    if w < 2:
+        g.sync.wait_ge(T.sem.copied, 16)
+    g.sync.wait_ge(T.sem.arrived, 8 * (len(cores) - 1))
+    g.sync.dma_start(T.y[:], T.land[:]).then_inc(T.sem.stored, 16)
+
+    g.wait_ge(T.sem.sent, 16)
+    g.wait_ge(T.sem.stored, 16)

@@ -1,15 +1,16 @@
 from concourse.bass import DstId, RemoteDMATransfer
 
-SCRATCH = {
-    "land": ("sbuf", [128, 33], "float32"),
-    "stage": ("sbuf", [128, 4], "float32"),
-    "relay": ("sbuf", [128, 4], "float32"),
-}
-SEMAPHORES = ["loaded", "copied", "arrived", "sent", "stored"]
+XW = 4
+YW = 33
+PER = 2
+FORWARDERS = [6, 2, 3, 7]
 
-LOW8 = 0x00FF
-HIGH8 = 0xFF00
-RELAY_CORE = 6
+SCRATCH = {"land": ("sbuf", [128, YW], "float32")}
+for _w in range(1, XW + 1):
+    SCRATCH["blk%d" % _w] = ("dram", [128, _w], "float32")
+    SCRATCH["slot%d" % _w] = ("dram", [PER, 128, _w], "float32")
+
+SEMAPHORES = ["packed", "own", "arrived", "sent", "stored"]
 
 
 def _dst(topo, c):
@@ -17,60 +18,90 @@ def _dst(topo, c):
     return DstId(rid=rid, pnc=pid)
 
 
+def _bits(first, n):
+    return ((1 << n) - 1) << first
+
+
+def _deal(cores, widths, topo, parity):
+    srcs = sorted([r for r, c in enumerate(cores) if (topo.chip(c) & 1) == parity], key=lambda r: (-widths[r], r))
+    return [srcs[i * PER:(i + 1) * PER] for i in range(len(FORWARDERS))]
+
+
+def _engines(ranks, widths, r):
+    n = len([q for q in ranks if widths[q] == widths[r]])
+    e = 8
+    while e * n > 8:
+        e //= 2
+    return e
+
+
 def rank_program(g, core, T, topo):
     widths = T.tables["WIDTHS"]
     cores = list(T.cores)
     off = [sum(widths[:r]) for r in range(len(cores))]
     chip = topo.chip(core)
+    parity = chip & 1
     rank = T.rank_of(core)
+    rank_on = {topo.chip(c): c for c in cores}
 
     if rank is None:
-        if core % 8 != RELAY_CORE:
+        if core % 8 not in FORWARDERS or chip not in rank_on:
             return
-        owners = [r for r, c in enumerate(cores) if topo.chip(c) == chip]
-        if not owners:
+        ranks = _deal(cores, widths, topo, parity)[FORWARDERS.index(core % 8)]
+        if not ranks:
             return
-        r = owners[0]
-        w, o = widths[r], off[r]
-        far = [c for c in cores if (topo.chip(c) & 1) != (chip & 1)]
-        g.wait_ge(T.sem.arrived, 8)
-        g.remote_dma_fused(
-            [RemoteDMATransfer(src=T.relay[:, 0:w],
-                               dsts=[T.land[:, o:o + w] for _ in far],
-                               dst_ids=[_dst(topo, c) for c in far],
-                               dma_engine_mask=LOW8, remote_sem=T.sem.arrived)],
-            local_sem=T.sem.sent)
-        g.wait_ge(T.sem.sent, 8)
+        here, mate = rank_on[chip], rank_on[chip ^ 1]
+        g.wait_ge(T.sem.arrived, len(ranks))
+        left = 0
+        for w in sorted(set(widths[r] for r in ranks), reverse=True):
+            transfers = []
+            for i, r in enumerate([q for q in ranks if widths[q] == w]):
+                e = _engines(ranks, widths, r)
+                src = T["slot%d" % w][ranks.index(r)]
+                place = T.land[:, off[r]:off[r] + w]
+                transfers.append(RemoteDMATransfer(src=src, dst=place, dst_ids=[_dst(topo, mate)],
+                                                   dma_engine_mask=_bits(i * e, e), remote_sem=T.sem.arrived))
+                left += e
+                if cores[r] != here:
+                    transfers.append(RemoteDMATransfer(src=src, dst=place, dst_ids=[_dst(topo, here)],
+                                                       dma_engine_mask=_bits(8 + i * e, e), remote_sem=T.sem.arrived))
+                    left += e
+            g.remote_dma_fused(transfers, local_sem=T.sem.sent)
+        g.wait_ge(T.sem.sent, left)
         return
 
     w, o = widths[rank], off[rank]
+    blk = T["blk%d" % w]
     mine = T.land[:, o:o + w]
+    valid = T.x[:, 0:w]
     if w >= 2:
-        g.sync.dma_start(mine, T.x[:, 0:w]).then_inc(T.sem.loaded, 16)
-        src = mine
+        g.sync.dma_start(blk[:], valid).then_inc(T.sem.packed, 16)
+        g.scalar.dma_start(mine, valid).then_inc(T.sem.own, 16)
     else:
-        g.sync.dma_start(T.stage[:], T.x[:]).then_inc(T.sem.loaded, 16)
-        src = T.stage[:, 0:1]
-        g.scalar.wait_ge(T.sem.loaded, 16)
-        g.scalar.dma_start(mine, src).then_inc(T.sem.copied, 16)
+        g.dma_start(blk[:], valid, allow_slow_non_contiguous=True).then_inc(T.sem.packed, 16)
 
-    near = [c for c in cores if c != core and (topo.chip(c) & 1) == (chip & 1)]
-    relay = chip * 8 + RELAY_CORE
-    g.wait_ge(T.sem.loaded, 16)
-    g.remote_dma_fused(
-        [RemoteDMATransfer(src=src, dst=T.relay[:, 0:w], dst_ids=[_dst(topo, relay)],
-                           dma_engine_mask=HIGH8, remote_sem=T.sem.arrived),
-         RemoteDMATransfer(src=src,
-                           dsts=[T.land[:, o:o + w] for _ in near],
-                           dst_ids=[_dst(topo, c) for c in near],
-                           dma_engine_mask=LOW8, remote_sem=T.sem.arrived)],
-        local_sem=T.sem.sent)
-
-    g.sync.wait_ge(T.sem.loaded, 16)
+    deal = _deal(cores, widths, topo, parity)
+    f = [i for i, ranks in enumerate(deal) if rank in ranks][0]
+    slot = T["slot%d" % w][deal[f].index(rank)]
+    away = [ch * 8 + FORWARDERS[f] for ch in sorted(rank_on) if (ch & 1) == parity and ch != chip]
+    transfers = [RemoteDMATransfer(src=blk[:], dst=slot, dst_ids=[_dst(topo, chip * 8 + FORWARDERS[f])],
+                                   dma_engine_mask=_bits(8, 1), remote_sem=T.sem.arrived)]
+    for i, c in enumerate(away):
+        transfers.append(RemoteDMATransfer(src=blk[:], dst=slot, dst_ids=[_dst(topo, c)],
+                                           dma_engine_mask=_bits(i, 1), remote_sem=T.sem.arrived))
+    g.wait_ge(T.sem.packed, 16)
+    g.remote_dma_fused(transfers, local_sem=T.sem.sent)
     if w < 2:
-        g.sync.wait_ge(T.sem.copied, 16)
-    g.sync.wait_ge(T.sem.arrived, 8 * (len(cores) - 1))
+        g.dma_start(mine, valid, allow_slow_non_contiguous=True).then_inc(T.sem.own, 16)
+
+    due = 0
+    for par in (0, 1):
+        for ranks in _deal(cores, widths, topo, par):
+            due += sum(_engines(ranks, widths, r) for r in ranks if r != rank)
+
+    g.sync.wait_ge(T.sem.own, 16)
+    g.sync.wait_ge(T.sem.arrived, due)
     g.sync.dma_start(T.y[:], T.land[:]).then_inc(T.sem.stored, 16)
 
-    g.wait_ge(T.sem.sent, 16)
+    g.wait_ge(T.sem.sent, len(transfers))
     g.wait_ge(T.sem.stored, 16)

from concourse.bass import DstId, RemoteDMATransfer

XW = 4
YW = 33
PER = 2
FORWARDERS = [6, 2, 3, 7]

SCRATCH = {"land": ("sbuf", [128, YW], "float32")}
for _w in range(1, XW + 1):
    SCRATCH["blk%d" % _w] = ("dram", [128, _w], "float32")
    SCRATCH["slot%d" % _w] = ("dram", [PER, 128, _w], "float32")

SEMAPHORES = ["packed", "own", "arrived", "sent", "stored"]


def _dst(topo, c):
    rid, pid, _se = topo.addr(c)
    return DstId(rid=rid, pnc=pid)


def _bits(first, n):
    return ((1 << n) - 1) << first


def _deal(cores, widths, topo, parity):
    srcs = sorted([r for r, c in enumerate(cores) if (topo.chip(c) & 1) == parity], key=lambda r: (-widths[r], r))
    return [srcs[i * PER:(i + 1) * PER] for i in range(len(FORWARDERS))]


def _engines(ranks, widths, r):
    n = len([q for q in ranks if widths[q] == widths[r]])
    e = 8
    while e * n > 8:
        e //= 2
    return e


def rank_program(g, core, T, topo):
    widths = T.tables["WIDTHS"]
    cores = list(T.cores)
    off = [sum(widths[:r]) for r in range(len(cores))]
    chip = topo.chip(core)
    parity = chip & 1
    rank = T.rank_of(core)
    rank_on = {topo.chip(c): c for c in cores}

    if rank is None:
        if core % 8 not in FORWARDERS or chip not in rank_on:
            return
        ranks = _deal(cores, widths, topo, parity)[FORWARDERS.index(core % 8)]
        if not ranks:
            return
        here, mate = rank_on[chip], rank_on[chip ^ 1]
        g.wait_ge(T.sem.arrived, len(ranks))
        left = 0
        for w in sorted(set(widths[r] for r in ranks), reverse=True):
            transfers = []
            for i, r in enumerate([q for q in ranks if widths[q] == w]):
                e = _engines(ranks, widths, r)
                src = T["slot%d" % w][ranks.index(r)]
                place = T.land[:, off[r]:off[r] + w]
                transfers.append(RemoteDMATransfer(src=src, dst=place, dst_ids=[_dst(topo, mate)],
                                                   dma_engine_mask=_bits(i * e, e), remote_sem=T.sem.arrived))
                left += e
                if cores[r] != here:
                    transfers.append(RemoteDMATransfer(src=src, dst=place, dst_ids=[_dst(topo, here)],
                                                       dma_engine_mask=_bits(8 + i * e, e), remote_sem=T.sem.arrived))
                    left += e
            g.remote_dma_fused(transfers, local_sem=T.sem.sent)
        g.wait_ge(T.sem.sent, left)
        return

    w, o = widths[rank], off[rank]
    blk = T["blk%d" % w]
    mine = T.land[:, o:o + w]
    valid = T.x[:, 0:w]
    if w >= 2:
        g.sync.dma_start(blk[:], valid).then_inc(T.sem.packed, 16)
        g.scalar.dma_start(mine, valid).then_inc(T.sem.own, 16)
    else:
        g.dma_start(blk[:], valid, allow_slow_non_contiguous=True).then_inc(T.sem.packed, 16)

    deal = _deal(cores, widths, topo, parity)
    f = [i for i, ranks in enumerate(deal) if rank in ranks][0]
    slot = T["slot%d" % w][deal[f].index(rank)]
    away = [ch * 8 + FORWARDERS[f] for ch in sorted(rank_on) if (ch & 1) == parity and ch != chip]
    transfers = [RemoteDMATransfer(src=blk[:], dst=slot, dst_ids=[_dst(topo, chip * 8 + FORWARDERS[f])],
                                   dma_engine_mask=_bits(8, 1), remote_sem=T.sem.arrived)]
    for i, c in enumerate(away):
        transfers.append(RemoteDMATransfer(src=blk[:], dst=slot, dst_ids=[_dst(topo, c)],
                                           dma_engine_mask=_bits(i, 1), remote_sem=T.sem.arrived))
    g.wait_ge(T.sem.packed, 16)
    g.remote_dma_fused(transfers, local_sem=T.sem.sent)
    if w < 2:
        g.dma_start(mine, valid, allow_slow_non_contiguous=True).then_inc(T.sem.own, 16)

    due = 0
    for par in (0, 1):
        for ranks in _deal(cores, widths, topo, par):
            due += sum(_engines(ranks, widths, r) for r in ranks if r != rank)

    g.sync.wait_ge(T.sem.own, 16)
    g.sync.wait_ge(T.sem.arrived, due)
    g.sync.dma_start(T.y[:], T.land[:]).then_inc(T.sem.stored, 16)

    g.wait_ge(T.sem.sent, len(transfers))
    g.wait_ge(T.sem.stored, 16)
